import numpy as np, ml_dtypes
CORES = [242,247,114,119]
N = 4
C = 64
def setup_inputs(rng):
    u = np.triu(np.ones((128, 128), np.float32)).astype(ml_dtypes.bfloat16)
    return {"x": rng.standard_normal((N, 128, C), dtype=np.float32).astype(ml_dtypes.bfloat16), "u": np.broadcast_to(u, (N, 128, 128)).copy()}
def setup_inputs_big(rng):
    d = setup_inputs(rng)
    for k in ("x",): d[k] = (d[k].astype(np.float32) * 1048576.0).astype(d[k].dtype)
    return d
def setup_inputs_small(rng):
    d = setup_inputs(rng)
    for k in ("x",): d[k] = (d[k].astype(np.float32) * (1 / 1048576.0)).astype(d[k].dtype)
    return d
def setup_inputs_apart(rng):
    d = setup_inputs(rng)
    f = (10.0 ** rng.permutation(np.linspace(-1.5, 1.5, N))).astype(np.float32).reshape(N, 1, 1)
    for k in ("x",): d[k] = (d[k].astype(np.float32) * f).astype(d[k].dtype)
    return d
def reference(x, u):
    X, U = x.astype(np.float64), u.astype(np.float64)
    y = np.zeros((N, 128, C)); c = np.zeros(C)
    for r in range(N):
        y[r] = U[r].T @ X[r] + c
        c = c + X[r].sum(axis=0)
    return {"y": y.astype(ml_dtypes.bfloat16 if x.dtype != np.float64 else np.float64)}

@@ -1,0 +1,82 @@
+from concourse.bass import DstId, RemoteDMATransfer
+
+N, C = 4, 64
+
+SCRATCH = {
+    "xs": ("sbuf", [128, C], "bfloat16"),
+    "us": ("sbuf", [128, 128], "bfloat16"),
+    "ones": ("sbuf", [128, 128], "bfloat16"),
+    "land": ("sbuf", [128, (N - 1) * C], "bfloat16"),
+    "acc": ("psum", [128, C], "float32"),
+    "ys": ("sbuf", [128, C], "bfloat16"),
+}
+SEMAPHORES = ["xl", "ul", "filled", "arrived", "sent", "mm", "copied", "stored"]
+
+
+def _engines_per_write(n_dsts):
+    return 8 if n_dsts == 1 else 4
+
+
+def _bits(m):
+    return [e for e in range(m.bit_length()) if (m >> e) & 1]
+
+
+def _masks(core, dsts, k, topo):
+    allowed = {d: _bits(topo.mask(core, d)) for d in dsts}
+    todo = sorted(dsts, key=lambda d: len(allowed[d]))
+    used, out = set(), {}
+    while todo:
+        d = todo.pop(0)
+        cand = sorted((e for e in allowed[d] if e not in used),
+                      key=lambda e: (sum(e in allowed[o] for o in todo), e))
+        step = 2 if len(cand) >= 2 * k else 1
+        pick = cand[0:step * k:step]
+        assert len(pick) == k
+        used.update(pick)
+        out[d] = sum(1 << e for e in pick)
+    return out
+
+
+def rank_program(g, core, T, topo):
+    r = T.rank_of(core)
+    if r is None:
+        return
+    S = T.sem
+    later = [T.cores[s] for s in range(r + 1, N)]
+
+    g.sync.dma_start(T.xs[:, :], T.x[:, :]).then_inc(S.xl, 16)
+    g.sync.dma_start(T.us[:, :], T.u[:, :]).then_inc(S.ul, 16)
+    if r > 0:
+        g.vector.memset(T.ones[:, :], 1.0).then_inc(S.filled, 1)
+
+    if later:
+        k = _engines_per_write(len(later))
+        masks = _masks(core, later, k, topo)
+        transfers = []
+        for d in later:
+            assert topo.may_write(core, d)
+            rid, pid = topo.addr(d, core)
+            transfers.append(RemoteDMATransfer(
+                dst_ids=[DstId(rid=rid, pnc=pid)], dma_engine_mask=masks[d], remote_sem=S.arrived,
+                src=T.xs[:, :], dst=T.land[:, r * C:(r + 1) * C]))
+        g.wait_ge(S.xl, 16)
+        g.remote_dma_fused(transfers, local_sem=S.sent)
+
+    g.tensor.wait_ge(S.xl, 16)
+    g.tensor.wait_ge(S.ul, 16)
+    g.tensor.matmul(T.acc[:, :], T.us[:, :], T.xs[:, :], start=True, stop=(r == 0)).then_inc(S.mm, 1)
+    if r > 0:
+        g.tensor.wait_ge(S.filled, 1)
+        g.tensor.wait_ge(S.arrived, sum(_engines_per_write(N - 1 - s) for s in range(r)))
+        for s in range(r):
+            g.tensor.matmul(T.acc[:, :], T.ones[:, :], T.land[:, s * C:(s + 1) * C],
+                            start=False, stop=(s == r - 1)).then_inc(S.mm, 1)
+
+    g.vector.wait_ge(S.mm, r + 1)
+    g.vector.tensor_copy(T.ys[:, :], T.acc[:, :]).then_inc(S.copied, 1)
+    g.sync.wait_ge(S.copied, 1)
+    g.sync.dma_start(T.y[:, :], T.ys[:, :]).then_inc(S.stored, 16)
+    g.sync.wait_ge(S.stored, 16)
+
+    if later:
+        g.wait_ge(S.sent, len(later) * _engines_per_write(len(later)))

@@ -1,8 +1,8 @@
-from concourse.bass import DstId, RemoteDMATransfer
-
 N, C = 4, 64
+K = 8
 
 SCRATCH = {
+    "xd": ("dram", [128, C], "bfloat16"),
     "xs": ("sbuf", [128, C], "bfloat16"),
     "us": ("sbuf", [128, 128], "bfloat16"),
     "ones": ("sbuf", [128, 128], "bfloat16"),
@@ -10,31 +10,30 @@ SCRATCH = {
     "acc": ("psum", [128, C], "float32"),
     "ys": ("sbuf", [128, C], "bfloat16"),
 }
-SEMAPHORES = ["xl", "ul", "filled", "arrived", "sent", "mm", "copied", "stored"]
-
-
-def _engines_per_write(n_dsts):
-    return 8 if n_dsts == 1 else 4
+SEMAPHORES = ["xc", "xl", "ul", "filled", "sent", "mm", "copied", "stored"] + ["arr%d" % s for s in range(N - 1)]
 
 
 def _bits(m):
     return [e for e in range(m.bit_length()) if (m >> e) & 1]
 
 
-def _masks(core, dsts, k, topo):
-    allowed = {d: _bits(topo.mask(core, d)) for d in dsts}
-    todo = sorted(dsts, key=lambda d: len(allowed[d]))
-    used, out = set(), {}
-    while todo:
-        d = todo.pop(0)
-        cand = sorted((e for e in allowed[d] if e not in used),
-                      key=lambda e: (sum(e in allowed[o] for o in todo), e))
-        step = 2 if len(cand) >= 2 * k else 1
-        pick = cand[0:step * k:step]
-        assert len(pick) == k
-        used.update(pick)
-        out[d] = sum(1 << e for e in pick)
-    return out
+def _mask(core, d, dsts, k, topo):
+    others = [_bits(topo.mask(core, o)) for o in dsts if o != d]
+    cand = sorted(_bits(topo.mask(core, d)), key=lambda e: (sum(e in a for a in others), e))
+    step = 2 if not others and len(cand) >= 2 * k else 1
+    pick = cand[0:step * k:step]
+    assert len(pick) == k
+    return sum(1 << e for e in pick)
+
+
+def _served(s, cores, topo):
+    me = cores[s]
+
+    def key(q):
+        d = cores[q]
+        same_chip = (topo.host(d), topo.chip(d)) == (topo.host(me), topo.chip(me))
+        return (same_chip, topo.die(d) == topo.die(me), q)
+    return sorted(range(s + 1, N), key=key)
 
 
 def rank_program(g, core, T, topo):
@@ -42,35 +41,34 @@ def rank_program(g, core, T, topo):
     if r is None:
         return
     S = T.sem
-    later = [T.cores[s] for s in range(r + 1, N)]
+    served = _served(r, T.cores, topo)
+    later = [T.cores[q] for q in served]
 
+    if later:
+        g.sync.dma_start(T.xd[:, :], T.x[:, :]).then_inc(S.xc, 16)
     g.sync.dma_start(T.xs[:, :], T.x[:, :]).then_inc(S.xl, 16)
     g.sync.dma_start(T.us[:, :], T.u[:, :]).then_inc(S.ul, 16)
     if r > 0:
         g.vector.memset(T.ones[:, :], 1.0).then_inc(S.filled, 1)
 
     if later:
-        k = _engines_per_write(len(later))
-        masks = _masks(core, later, k, topo)
-        transfers = []
+        g.wait_ge(S.xc, 16)
         for d in later:
             assert topo.may_write(core, d)
             rid, pid = topo.addr(d, core)
-            transfers.append(RemoteDMATransfer(
-                dst_ids=[DstId(rid=rid, pnc=pid)], dma_engine_mask=masks[d], remote_sem=S.arrived,
-                src=T.xs[:, :], dst=T.land[:, r * C:(r + 1) * C]))
-        g.wait_ge(S.xl, 16)
-        g.remote_dma_fused(transfers, local_sem=S.sent)
+            g.remote_dma(T.land[:, r * C:(r + 1) * C], T.xd[:, :], S["arr%d" % r], S.sent, pid, rid,
+                         _mask(core, d, later, K, topo))
 
     g.tensor.wait_ge(S.xl, 16)
     g.tensor.wait_ge(S.ul, 16)
     g.tensor.matmul(T.acc[:, :], T.us[:, :], T.xs[:, :], start=True, stop=(r == 0)).then_inc(S.mm, 1)
     if r > 0:
         g.tensor.wait_ge(S.filled, 1)
-        g.tensor.wait_ge(S.arrived, sum(_engines_per_write(N - 1 - s) for s in range(r)))
-        for s in range(r):
+        senders = sorted(range(r), key=lambda s: (_served(s, T.cores, topo).index(r), -s))
+        for s in senders:
+            g.tensor.wait_ge(S["arr%d" % s], K)
             g.tensor.matmul(T.acc[:, :], T.ones[:, :], T.land[:, s * C:(s + 1) * C],
-                            start=False, stop=(s == r - 1)).then_inc(S.mm, 1)
+                            start=False, stop=(s == senders[-1])).then_inc(S.mm, 1)
 
     g.vector.wait_ge(S.mm, r + 1)
     g.vector.tensor_copy(T.ys[:, :], T.acc[:, :]).then_inc(S.copied, 1)
@@ -79,4 +77,4 @@ def rank_program(g, core, T, topo):
     g.sync.wait_ge(S.stored, 16)
 
     if later:
-        g.wait_ge(S.sent, len(later) * _engines_per_write(len(later)))
+        g.wait_ge(S.sent, len(later) * K)

N, C = 4, 64
K = 8

SCRATCH = {
    "xd": ("dram", [128, C], "bfloat16"),
    "xs": ("sbuf", [128, C], "bfloat16"),
    "us": ("sbuf", [128, 128], "bfloat16"),
    "ones": ("sbuf", [128, 128], "bfloat16"),
    "land": ("sbuf", [128, (N - 1) * C], "bfloat16"),
    "acc": ("psum", [128, C], "float32"),
    "ys": ("sbuf", [128, C], "bfloat16"),
}
SEMAPHORES = ["xc", "xl", "ul", "filled", "sent", "mm", "copied", "stored"] + ["arr%d" % s for s in range(N - 1)]


def _bits(m):
    return [e for e in range(m.bit_length()) if (m >> e) & 1]


def _mask(core, d, dsts, k, topo):
    others = [_bits(topo.mask(core, o)) for o in dsts if o != d]
    cand = sorted(_bits(topo.mask(core, d)), key=lambda e: (sum(e in a for a in others), e))
    step = 2 if not others and len(cand) >= 2 * k else 1
    pick = cand[0:step * k:step]
    assert len(pick) == k
    return sum(1 << e for e in pick)


def _served(s, cores, topo):
    me = cores[s]

    def key(q):
        d = cores[q]
        same_chip = (topo.host(d), topo.chip(d)) == (topo.host(me), topo.chip(me))
        return (same_chip, topo.die(d) == topo.die(me), q)
    return sorted(range(s + 1, N), key=key)


def rank_program(g, core, T, topo):
    r = T.rank_of(core)
    if r is None:
        return
    S = T.sem
    served = _served(r, T.cores, topo)
    later = [T.cores[q] for q in served]

    if later:
        g.sync.dma_start(T.xd[:, :], T.x[:, :]).then_inc(S.xc, 16)
    g.sync.dma_start(T.xs[:, :], T.x[:, :]).then_inc(S.xl, 16)
    g.sync.dma_start(T.us[:, :], T.u[:, :]).then_inc(S.ul, 16)
    if r > 0:
        g.vector.memset(T.ones[:, :], 1.0).then_inc(S.filled, 1)

    if later:
        g.wait_ge(S.xc, 16)
        for d in later:
            assert topo.may_write(core, d)
            rid, pid = topo.addr(d, core)
            g.remote_dma(T.land[:, r * C:(r + 1) * C], T.xd[:, :], S["arr%d" % r], S.sent, pid, rid,
                         _mask(core, d, later, K, topo))

    g.tensor.wait_ge(S.xl, 16)
    g.tensor.wait_ge(S.ul, 16)
    g.tensor.matmul(T.acc[:, :], T.us[:, :], T.xs[:, :], start=True, stop=(r == 0)).then_inc(S.mm, 1)
    if r > 0:
        g.tensor.wait_ge(S.filled, 1)
        senders = sorted(range(r), key=lambda s: (_served(s, T.cores, topo).index(r), -s))
        for s in senders:
            g.tensor.wait_ge(S["arr%d" % s], K)
            g.tensor.matmul(T.acc[:, :], T.ones[:, :], T.land[:, s * C:(s + 1) * C],
                            start=False, stop=(s == senders[-1])).then_inc(S.mm, 1)

    g.vector.wait_ge(S.mm, r + 1)
    g.vector.tensor_copy(T.ys[:, :], T.acc[:, :]).then_inc(S.copied, 1)
    g.sync.wait_ge(S.copied, 1)
    g.sync.dma_start(T.y[:, :], T.ys[:, :]).then_inc(S.stored, 16)
    g.sync.wait_ge(S.stored, 16)

    if later:
        g.wait_ge(S.sent, len(later) * K)
